import numpy as np
import ml_dtypes

BF16 = ml_dtypes.bfloat16


def bf(x):
    return np.asarray(x, np.float32).astype(BF16)


def f32(x):
    return np.asarray(x, np.float32)


def f64(x):
    return np.asarray(x).astype(np.float64)


def striped(idx):
    return np.concatenate([l.reshape(-1, 16).T for l in idx])


def rows(idx, k):
    return np.tile(np.repeat(idx, 16, axis=0), (k // (16 * 8), 1))


def look(tab, idx):
    return np.take_along_axis(f64(tab), rows(idx, len(tab)), axis=1)


K, S, D, V, N, M = 256, 2048, 2, 512, 1024, 512


def setup_inputs():
    return {"tab": f32(np.random.standard_normal((K, S))), "ctr": f32(np.random.standard_normal((K, V))), "w": bf(np.random.standard_normal((K, M)) / np.sqrt(K)), "b": f32(0.5 * np.random.standard_normal((M, 1))), "offs": striped(np.stack([np.random.permutation(S)[:N] for _ in range(8)]))}


def reference(tab, ctr, w, b, offs):
    idx = np.stack([g.T.reshape(-1) for g in np.split(offs, 8)])
    x = sum(np.maximum(look(tab, idx[:, d * V:(d + 1) * V]) - f64(ctr), 0.0) for d in range(D))
    y = f64(w).T @ x
    return np.maximum(y + f64(b), 0.0)

@@ -1,0 +1,65 @@
+import concourse.mybir as mybir
+
+FLOPS = 2 * 256 * 512 * 512 + 3 * 2 * 256 * 512
+
+F32, BF16, U16 = mybir.dt.float32, mybir.dt.bfloat16, mybir.dt.uint16
+ADD, MAX, SUBTRACT = mybir.AluOpType.add, mybir.AluOpType.max, mybir.AluOpType.subtract
+RELU = mybir.ActivationFunctionType.Relu
+
+P = 128
+R = 256 // P
+S = 2048
+D = 2
+V = 512
+M = 512
+Q = M // P
+COLS = V // 16
+
+
+def tile_lookup_edge_sub_relu_kernel(tc, tab, ctr, w, b, offs, out):
+    nc = tc.nc
+    with (
+        tc.tile_pool(name="held", bufs=1) as held,
+        tc.tile_pool(name="work", bufs=2) as work,
+        tc.psum_pool(name="psum", bufs=1) as psum,
+    ):
+        offsets = held.tile([P, D * COLS], U16)
+        nc.sync.dma_start(offsets[:], offs)
+
+        tab_tiles, ctr_tiles, w_tiles = [], [], []
+        for r in range(R):
+            rows = slice(r * P, (r + 1) * P)
+            window = held.tile([P, S], F32, name=f"window{r}")
+            nc.sync.dma_start(window[:], tab[rows, :])
+            centre = held.tile([P, V], F32, name=f"centre{r}")
+            nc.sync.dma_start(centre[:], ctr[rows, :])
+            weights = held.tile([P, M], BF16, name=f"weights{r}")
+            nc.sync.dma_start(weights[:], w[rows, :])
+            tab_tiles.append(window)
+            ctr_tiles.append(centre)
+            w_tiles.append(weights)
+
+        bias = held.tile([P, Q], F32)
+        nc.sync.dma_start(bias[:], b.rearrange("(p q) one -> p (q one)", q=Q))
+
+        banks = [psum.tile([P, V], F32, name=f"bank{q}") for q in range(Q)]
+        for r in range(R):
+            diff = [work.tile([P, V], F32, name=f"diff{d}") for d in range(D)]
+            for d in range(D):
+                neighbours = tab_tiles[r][:].indirect(offsets[:, d * COLS : (d + 1) * COLS])
+                nc.vector.tensor_tensor(diff[d][:], neighbours, ctr_tiles[r][:], SUBTRACT)
+            positive0 = work.tile([P, V], F32)
+            nc.scalar.activation(positive0[:], diff[0][:], RELU)
+            x = work.tile([P, V], BF16)
+            nc.vector.scalar_tensor_tensor(x[:], diff[1][:], 0.0, positive0[:], MAX, ADD)
+            for q in range(Q):
+                nc.tensor.matmul(banks[q][:], w_tiles[r][:, q::Q], x[:], start=r == 0, stop=r == R - 1)
+
+        out_groups = out.rearrange("(p q) j -> p q j", q=Q)
+        for q in range(Q):
+            result = held.tile([P, V], F32, name=f"result{q}")
+            if q % 2 == 0:
+                nc.scalar.activation(result[:], banks[q][:], RELU, bias=bias[:, q : q + 1])
+            else:
+                nc.vector.tensor_scalar(result[:], banks[q][:], bias[:, q : q + 1], 0.0, ADD, MAX)
+            nc.sync.dma_start(out_groups[:, q, :], result[:])

@@ -26,18 +26,17 @@ def tile_lookup_edge_sub_relu_kernel(tc, tab, ctr, w, b, offs, out):
         offsets = held.tile([P, D * COLS], U16)
         nc.sync.dma_start(offsets[:], offs)
 
-        tab_tiles, ctr_tiles, w_tiles = [], [], []
+        tab_tiles, ctr_tiles = [], []
         for r in range(R):
             rows = slice(r * P, (r + 1) * P)
             window = held.tile([P, S], F32, name=f"window{r}")
             nc.sync.dma_start(window[:], tab[rows, :])
             centre = held.tile([P, V], F32, name=f"centre{r}")
             nc.sync.dma_start(centre[:], ctr[rows, :])
-            weights = held.tile([P, M], BF16, name=f"weights{r}")
-            nc.sync.dma_start(weights[:], w[rows, :])
             tab_tiles.append(window)
             ctr_tiles.append(centre)
-            w_tiles.append(weights)
+        weights = held.tile([P, R, M], BF16)
+        nc.sync.dma_start(weights[:], w.rearrange("(r p) m -> p r m", p=P))
 
         bias = held.tile([P, Q], F32)
         nc.sync.dma_start(bias[:], b.rearrange("(p q) one -> p (q one)", q=Q))
@@ -53,7 +52,7 @@ def tile_lookup_edge_sub_relu_kernel(tc, tab, ctr, w, b, offs, out):
             x = work.tile([P, V], BF16)
             nc.vector.scalar_tensor_tensor(x[:], diff[1][:], 0.0, positive0[:], MAX, ADD)
             for q in range(Q):
-                nc.tensor.matmul(banks[q][:], w_tiles[r][:, q::Q], x[:], start=r == 0, stop=r == R - 1)
+                nc.tensor.matmul(banks[q][:], weights[:, r, q::Q], x[:], start=r == 0, stop=r == R - 1)
 
         out_groups = out.rearrange("(p q) j -> p q j", q=Q)
         for q in range(Q):

@@ -13,6 +13,9 @@ D = 2
 V = 512
 M = 512
 Q = M // P
+H = 2
+VH = V // H
+WARM = 24
 COLS = V // 16
 
 
@@ -41,7 +44,14 @@ def tile_lookup_edge_sub_relu_kernel(tc, tab, ctr, w, b, offs, out):
         bias = held.tile([P, Q], F32)
         nc.sync.dma_start(bias[:], b.rearrange("(p q) one -> p (q one)", q=Q))
 
-        banks = [psum.tile([P, V], F32, name=f"bank{q}") for q in range(Q)]
+        banks = [[psum.tile([P, V], F32, name=f"bank{q}_{h}") for h in range(H)] for q in range(Q)]
+
+        zeros = held.tile([P, V], BF16)
+        nc.gpsimd.memset(zeros[:], 0.0)
+        for i in range(WARM):
+            nc.tensor.matmul(banks[0][0][:], zeros[:, :P], zeros[:], start=True, stop=True)
+
+        halves = [slice(h * VH, (h + 1) * VH) for h in range(H)]
         for r in range(R):
             diff = [work.tile([P, V], F32, name=f"diff{d}") for d in range(D)]
             for d in range(D):
@@ -49,16 +59,20 @@ def tile_lookup_edge_sub_relu_kernel(tc, tab, ctr, w, b, offs, out):
                 nc.vector.tensor_tensor(diff[d][:], neighbours, ctr_tiles[r][:], SUBTRACT)
             positive0 = work.tile([P, V], F32)
             nc.scalar.activation(positive0[:], diff[0][:], RELU)
-            x = work.tile([P, V], BF16)
-            nc.vector.scalar_tensor_tensor(x[:], diff[1][:], 0.0, positive0[:], MAX, ADD)
-            for q in range(Q):
-                nc.tensor.matmul(banks[q][:], weights[:, r, q::Q], x[:], start=r == 0, stop=r == R - 1)
+            for h, cols in enumerate(halves):
+                x = work.tile([P, VH], BF16, name=f"x{h}")
+                nc.vector.scalar_tensor_tensor(x[:], diff[1][:, cols], 0.0, positive0[:, cols], MAX, ADD)
+                for q in range(Q):
+                    nc.tensor.matmul(
+                        banks[q][h][:, :VH], weights[:, r, q::Q], x[:], start=r == 0, stop=r == R - 1
+                    )
 
         out_groups = out.rearrange("(p q) j -> p q j", q=Q)
-        for q in range(Q):
-            result = held.tile([P, V], F32, name=f"result{q}")
-            if q % 2 == 0:
-                nc.scalar.activation(result[:], banks[q][:], RELU, bias=bias[:, q : q + 1])
-            else:
-                nc.vector.tensor_scalar(result[:], banks[q][:], bias[:, q : q + 1], 0.0, ADD, MAX)
-            nc.sync.dma_start(out_groups[:, q, :], result[:])
+        for h, cols in enumerate(halves):
+            for q in range(Q):
+                result = held.tile([P, VH], F32, name=f"result{q}_{h}")
+                if q % 2 == 0:
+                    nc.scalar.activation(result[:], banks[q][h][:, :VH], RELU, bias=bias[:, q : q + 1])
+                else:
+                    nc.vector.tensor_scalar(result[:], banks[q][h][:, :VH], bias[:, q : q + 1], 0.0, ADD, MAX)
+                nc.sync.dma_start(out_groups[:, q, cols], result[:])

import concourse.mybir as mybir

FLOPS = 2 * 256 * 512 * 512 + 3 * 2 * 256 * 512

F32, BF16, U16 = mybir.dt.float32, mybir.dt.bfloat16, mybir.dt.uint16
ADD, MAX, SUBTRACT = mybir.AluOpType.add, mybir.AluOpType.max, mybir.AluOpType.subtract
RELU = mybir.ActivationFunctionType.Relu

P = 128
R = 256 // P
S = 2048
D = 2
V = 512
M = 512
Q = M // P
H = 2
VH = V // H
WARM = 24
COLS = V // 16


def tile_lookup_edge_sub_relu_kernel(tc, tab, ctr, w, b, offs, out):
    nc = tc.nc
    with (
        tc.tile_pool(name="held", bufs=1) as held,
        tc.tile_pool(name="work", bufs=2) as work,
        tc.psum_pool(name="psum", bufs=1) as psum,
    ):
        offsets = held.tile([P, D * COLS], U16)
        nc.sync.dma_start(offsets[:], offs)

        tab_tiles, ctr_tiles = [], []
        for r in range(R):
            rows = slice(r * P, (r + 1) * P)
            window = held.tile([P, S], F32, name=f"window{r}")
            nc.sync.dma_start(window[:], tab[rows, :])
            centre = held.tile([P, V], F32, name=f"centre{r}")
            nc.sync.dma_start(centre[:], ctr[rows, :])
            tab_tiles.append(window)
            ctr_tiles.append(centre)
        weights = held.tile([P, R, M], BF16)
        nc.sync.dma_start(weights[:], w.rearrange("(r p) m -> p r m", p=P))

        bias = held.tile([P, Q], F32)
        nc.sync.dma_start(bias[:], b.rearrange("(p q) one -> p (q one)", q=Q))

        banks = [[psum.tile([P, V], F32, name=f"bank{q}_{h}") for h in range(H)] for q in range(Q)]

        zeros = held.tile([P, V], BF16)
        nc.gpsimd.memset(zeros[:], 0.0)
        for i in range(WARM):
            nc.tensor.matmul(banks[0][0][:], zeros[:, :P], zeros[:], start=True, stop=True)

        halves = [slice(h * VH, (h + 1) * VH) for h in range(H)]
        for r in range(R):
            diff = [work.tile([P, V], F32, name=f"diff{d}") for d in range(D)]
            for d in range(D):
                neighbours = tab_tiles[r][:].indirect(offsets[:, d * COLS : (d + 1) * COLS])
                nc.vector.tensor_tensor(diff[d][:], neighbours, ctr_tiles[r][:], SUBTRACT)
            positive0 = work.tile([P, V], F32)
            nc.scalar.activation(positive0[:], diff[0][:], RELU)
            for h, cols in enumerate(halves):
                x = work.tile([P, VH], BF16, name=f"x{h}")
                nc.vector.scalar_tensor_tensor(x[:], diff[1][:, cols], 0.0, positive0[:, cols], MAX, ADD)
                for q in range(Q):
                    nc.tensor.matmul(
                        banks[q][h][:, :VH], weights[:, r, q::Q], x[:], start=r == 0, stop=r == R - 1
                    )

        out_groups = out.rearrange("(p q) j -> p q j", q=Q)
        for h, cols in enumerate(halves):
            for q in range(Q):
                result = held.tile([P, VH], F32, name=f"result{q}_{h}")
                if q % 2 == 0:
                    nc.scalar.activation(result[:], banks[q][h][:, :VH], RELU, bias=bias[:, q : q + 1])
                else:
                    nc.vector.tensor_scalar(result[:], banks[q][h][:, :VH], bias[:, q : q + 1], 0.0, ADD, MAX)
                nc.sync.dma_start(out_groups[:, q, cols], result[:])
